import numpy as np
import ml_dtypes


def mxq(x, axis, fmt="e4m3"):
    dtype, down = {"e4m3": (ml_dtypes.float8_e4m3fn, 7), "e5m2": (ml_dtypes.float8_e5m2, 14)}[fmt]
    v = np.moveaxis(np.asarray(x, np.float32).astype(ml_dtypes.bfloat16).astype(np.float64), axis, -1)
    blocks = v.reshape(v.shape[:-1] + (-1, 32))
    amax = np.abs(blocks).max(-1, keepdims=True)
    byte = np.maximum(np.where(amax > 0, np.frexp(amax)[1] - 1 + 127, 0) - down, 1)
    scale = np.exp2(byte - 127.0)
    codes = (blocks / scale).astype(np.float32).astype(dtype).astype(np.float64)
    return np.moveaxis((codes * scale).reshape(v.shape), -1, axis)


WIDE = False


def mx_kscale(k):
    if not WIDE:
        return np.ones(k)
    levels = np.array([10, -10, 5, -5, 0])
    if k % 512:
        return np.exp2(np.random.permutation(np.resize(levels, k // 32))).repeat(32)
    a = np.empty((k // 512, 16))
    for p in range(k // 512):
        a[p, :8] = np.random.permutation(np.resize(levels, 8))
        for g in range(8):
            far = levels[np.abs(levels - a[p, g]) >= 10]
            a[p, g + 8] = far[np.random.randint(len(far))]
    return np.exp2(a.ravel()).repeat(32)


def f64(x):
    return np.asarray(x).astype(np.float64)


def striped(idx):
    return np.tile(idx.reshape(-1, 16).T, (8, 1)).astype(np.uint16)


def unstriped(offs):
    return offs[:16].T.reshape(-1).astype(np.int64)


E2M1 = np.array([0.0, 0.5, 1.0, 1.5, 2.0, 3.0, 4.0, 6.0, -0.0, -0.5, -1.0, -1.5, -2.0, -3.0, -4.0, -6.0])


def pack_weight(w, fmt):
    k, n = w.shape
    w = f64(np.asarray(w, np.float32).astype(ml_dtypes.bfloat16)).reshape(k // 32, 32, n)
    amax = np.abs(w).max(1)
    if fmt == "e4m3":
        byte = np.frexp(amax)[1] - 1 + 127 - 7
    else:
        mant, ex = np.frexp(amax / 6.0)
        byte = np.where(mant > 0.5, ex, ex - 1) + 127
    byte = np.clip(np.where(amax > 0, byte, 1), 1, 254)
    scaled = (w * np.exp2(127.0 - byte)[:, None, :]).reshape(k, n).astype(np.float32)
    by_word = np.ascontiguousarray(scaled.reshape(k // 512, 128, 4, n).transpose(0, 1, 3, 2))
    if fmt == "e4m3":
        words = by_word.astype(ml_dtypes.float8_e4m3fn).view(np.uint8)
    else:
        c = by_word.astype(ml_dtypes.float4_e2m1fn).view(np.uint8) & 0xF
        words = (c[..., 0::2] | (c[..., 1::2] << 4)).reshape(k // 512, 128, 2 * n)
    return np.ascontiguousarray(words), np.ascontiguousarray(byte.astype(np.uint8).reshape(k // 512, 16, n))


def unpack_weight(words, scales, fmt):
    g, _, n = scales.shape
    words = np.ascontiguousarray(words).reshape(g, 128, n, -1)
    if fmt == "e4m3":
        vals = words.view(ml_dtypes.float8_e4m3fn).astype(np.float64)
    else:
        nib = np.empty((g, 128, n, 4), np.uint8)
        nib[..., 0::2] = words & 0xF
        nib[..., 1::2] = words >> 4
        vals = E2M1[nib]
    vals = vals * np.repeat(np.exp2(scales.astype(np.float64) - 127.0), 8, axis=1)[..., None]
    return vals.transpose(0, 1, 3, 2).reshape(g * 512, n)


def gelu(v):
    return 0.5 * v * (1.0 + np.tanh(np.sqrt(2.0 / np.pi) * (v + 0.044715 * v**3)))


K, T, S, H, N, SPREAD, LEAN = 1024, 4096, 512, 1024, 768, 0.4, 0.85

def setup_inputs():
    n = np.random.standard_normal
    s = mx_kscale(K)[:, None]
    u = mx_kscale(H)[:, None]
    tab_words, tab_scales = pack_weight(n((K, T)) * s, "e4m3")
    wc = (n((K, H)) / np.sqrt(K) / s * u.T).astype(np.float32)
    wn_words, wn_scales = pack_weight(SPREAD * n((K, H)) / np.sqrt(K) / s, "e2m1")
    bn = np.random.uniform(-LEAN, LEAN, H).astype(np.float32)
    wo = (n((H, N)) / np.sqrt(H) / u).astype(np.float32)
    return {"tab_words": tab_words, "tab_scales": tab_scales,
            "offs": striped(np.random.permutation(T)[:S]),
            "offs2": striped(np.random.permutation(T)[:S]),
            "offs3": striped(np.random.permutation(T)[:S]),
            "wc": wc, "wn_words": wn_words, "wn_scales": wn_scales,
            "bn": bn, "wo": wo}

def reference(tab_words, tab_scales, offs, offs2, offs3, wc, wn_words, wn_scales, bn, wo):
    TW = unpack_weight(tab_words, tab_scales, "e4m3")
    v = TW[:, unstriped(offs)]
    v2 = TW[:, unstriped(offs2)]
    v3 = TW[:, unstriped(offs3)]
    wcq = mxq(f64(wc), 0, "e4m3")
    wn = unpack_weight(wn_words, wn_scales, "e2m1")
    first = wcq.T @ v
    second = wcq.T @ v2
    node = (wn.T @ v3) + f64(bn)[:, None]
    h = np.maximum(first, second) * np.sin(node) + np.minimum(first, second)
    hq = mxq(h, 0, "e4m3")
    return mxq(f64(wo), 0, "e4m3").T @ hq

@@ -1,0 +1,283 @@
+from contextlib import ExitStack
+
+import concourse.mybir as mybir
+
+K, T, S, H, N = 1024, 4096, 512, 1024, 768
+FLOPS = 2 * S * (3 * K * H + H * N)
+
+F32 = mybir.dt.float32
+BF16 = mybir.dt.bfloat16
+I32 = mybir.dt.int32
+U32 = mybir.dt.uint32
+U16 = mybir.dt.uint16
+U8 = mybir.dt.uint8
+E4M3 = mybir.dt.float8_e4m3fn_x4
+E2M1 = mybir.dt.float4_e2m1fn_x4
+ALU = mybir.AluOpType
+SIN = mybir.ActivationFunctionType.Sin
+
+P = 128
+PACK = 4
+KP = P * PACK
+BANK = 512
+RUN = 4
+
+
+def tile_list_modem_parent_features_kernel(
+    tc, tab_words, tab_scales, offs, offs2, offs3, wc, wn_words, wn_scales, bn, wo, out
+):
+    nc = tc.nc
+    with ExitStack() as ctx:
+        lists_pool = ctx.enter_context(tc.tile_pool(name="lists", bufs=1))
+        keep = ctx.enter_context(tc.tile_pool(name="keep", bufs=1))
+        ring = ctx.enter_context(tc.tile_pool(name="ring", bufs=2))
+        psum = ctx.enter_context(tc.psum_pool(name="psum", bufs=2))
+
+        tab_planes = keep.tile([P, T], U8, name="tab_planes", align_bytes=64)
+        nc.vector.memset(tab_planes[:].bitcast(I32), 0)
+        for q in range(4):
+            nc.scalar.dma_start(
+                out=tab_planes[32 * q : 32 * q + 8, :].bitcast(I32),
+                in_=tab_scales[:, 4 * q : 4 * q + 4, :].bitcast(I32),
+            )
+        lists = []
+        for n_list, source in enumerate((offs, offs2, offs3)):
+            tile = lists_pool.tile([P, S // 16], U16, name="list%d" % n_list)
+            nc.sync.dma_start(tile[:], source)
+            lists.append(tile)
+
+        bias = keep.tile([P, 2, 16], F32, name="bias")
+        bn_runs = bn.rearrange("(b u x) -> u b x", b=2, x=16)
+        for i in range(RUN):
+            nc.sync.dma_start(out=bias[i:P:RUN, :, 0:13], in_=bn_runs[:, :, i : i + 13])
+
+        wn_planes = keep.tile([P, 2, H], U8, name="wn_planes", align_bytes=64)
+        nc.gpsimd.memset(wn_planes[:].rearrange("p a c -> p (a c)").bitcast(I32), 0)
+        for q in range(4):
+            nc.gpsimd.dma_start(
+                out=wn_planes[32 * q : 32 * q + 4, :, :].bitcast(I32),
+                in_=wn_scales[:, 4 * q : 4 * q + 4, :].rearrange("a q c -> q a c").bitcast(I32),
+            )
+        node_plane1 = keep.tile([P, S], U8, name="node_plane1", align_bytes=64)
+        nc.gpsimd.memset(node_plane1[:].bitcast(I32), 0)
+
+        table = []
+        for a in range(2):
+            tile = keep.tile([P, T], I32, name="table%d" % a, align_bytes=64)
+            nc.sync.dma_start(out=tile[:], in_=tab_words[a].rearrange("p t i -> p (t i)").bitcast(I32))
+            table.append(tile)
+        wc_raw = {}
+        wn_raw = {}
+        wo_raw = {}
+
+        def load_wc(a, b):
+            tile = keep.tile([P, PACK, KP], F32, name="wc_raw%d%d" % (a, b))
+            nc.sync.dma_start(
+                out=tile[:],
+                in_=wc[a * KP : (a + 1) * KP, b * KP : (b + 1) * KP].rearrange("(p j) c -> p j c", j=PACK),
+            )
+            wc_raw[a, b] = tile
+
+        def load_wn(b):
+            tile = keep.tile([P, 2, KP // 2], I32, name="wn_raw%d" % b)
+            nc.sync.dma_start(
+                out=tile[:],
+                in_=wn_words[:, :, 2 * b * KP : 2 * (b + 1) * KP].rearrange("a p c -> p a c").bitcast(I32),
+            )
+            wn_raw[b] = tile
+
+        def load_wo(b):
+            tile = keep.tile([P, PACK, N], F32, name="wo_raw%d" % b)
+            rows = wo[b * KP : (b + 1) * KP, :].rearrange("(u t i) n -> t u i n", t=PACK, i=RUN)
+            for t in range(PACK):
+                nc.sync.dma_start(out=tile[:, t, :], in_=rows[t])
+            wo_raw[b] = tile
+
+        for b in range(2):
+            load_wc(0, b)
+            load_wn(b)
+            load_wc(1, b)
+        for b in range(2):
+            load_wo(b)
+
+        picked_planes = {}
+        for n_list in (2, 0, 1):
+            tile = keep.tile([P, S], U8, name="picked_planes%d" % n_list, align_bytes=64)
+            nc.vector.tensor_copy(out=tile[:], in_=tab_planes[:].indirect(lists[n_list][:]))
+            picked_planes[n_list] = tile
+        nc.gpsimd.dma_start(
+            out=node_plane1[0 : P - 4, :].bitcast(I32), in_=picked_planes[2][4:P, :].bitcast(I32)
+        )
+        picked = {}
+
+        def pick_words(a):
+            for n_list in range(3):
+                tile = keep.tile([P, S], U32, name="picked%d%d" % (n_list, a), align_bytes=64)
+                nc.vector.tensor_copy(out=tile[:], in_=table[a][:].bitcast(U32).indirect(lists[n_list][:]))
+                picked[n_list, a] = tile
+
+        pick_words(0)
+        wn_scale = keep.tile([P, 2, 2, PACK, P], U8, name="wn_scale", align_bytes=64)
+        nc.vector.tensor_copy(
+            out=wn_scale[:].bitcast(I32).rearrange("p a b t u -> p (a b) t u"),
+            in_=wn_planes[:].bitcast(I32).rearrange("p a (b u t) -> p (a b) t u", b=2, t=PACK),
+        )
+        pick_words(1)
+
+        wn_codes = {}
+
+        def deal_wn(b):
+            tile = keep.tile([P, 2, PACK, 2 * P], U8, name="wn_codes%d" % b, align_bytes=64)
+            nc.vector.tensor_copy(
+                out=tile[:].bitcast(I32).rearrange("p a t (u w) -> p a t u w", w=2),
+                in_=wn_raw[b][:].rearrange("p a (u t w) -> p a t u w", t=PACK, w=2),
+            )
+            wn_codes[b] = tile
+
+        wc_codes = {}
+
+        def round_wc(a, b, t, grouped, on_vector):
+            src_ap = wc_raw[a, b][:].rearrange("p j (u t i) -> p t u j i", t=PACK, i=RUN)[:, t]
+            dst_ap = grouped.rearrange("p (u i) j -> p u j i", i=RUN)
+            if on_vector:
+                nc.vector.tensor_copy(out=dst_ap, in_=src_ap)
+            else:
+                nc.scalar.copy(out=dst_ap, in_=src_ap)
+
+        def quantise(grouped, width, name):
+            codes = keep.tile([P, width], U32, name=name + "_codes", align_bytes=64)
+            scales = keep.tile([P, width], U8, name=name + "_scales", align_bytes=64)
+            nc.vector.quantize_mx(out=codes[:].bitcast(E4M3), scales=scales[:], in_=grouped)
+            return codes, scales
+
+        def make_wc(a, b, slots, on_vector):
+            grouped = ring.tile([P, len(slots), P, PACK], BF16, name="wc_grouped", tag="grouped", bufs=4, align_bytes=64)
+            for n_slot, t in enumerate(slots):
+                round_wc(a, b, t, grouped[:, n_slot], on_vector)
+            codes, scales = quantise(
+                grouped[:].rearrange("p s m j -> p (s m j)"), len(slots) * P, "wc%d%d%d" % (a, b, slots[0])
+            )
+            for n_slot, t in enumerate(slots):
+                cols = slice(n_slot * P, (n_slot + 1) * P)
+                wc_codes[a, b, t] = (codes[:, cols], scales[:, cols])
+
+        wo_codes = {}
+
+        def make_wo(b, pair):
+            grouped = ring.tile([P, 2, P, PACK], BF16, name="wo_grouped", tag="grouped", bufs=4, align_bytes=64)
+            for half in range(2):
+                n0 = (2 * pair + half) * P
+                nc.scalar.copy(
+                    out=grouped[:, half].rearrange("p (c i) t -> p c t i", i=4),
+                    in_=wo_raw[b][:, :, n0 : n0 + P].rearrange("p t (c i) -> p c t i", i=4),
+                )
+            codes, scales = quantise(grouped[:].rearrange("p s m j -> p (s m j)"), 2 * P, "wo%d%d" % (b, pair))
+            for half in range(2):
+                cols = slice(half * P, (half + 1) * P)
+                wo_codes[b, 2 * pair + half] = (codes[:, cols], scales[:, cols])
+
+        def scores(bank, cols, n_list, b, t, js):
+            for a in range(2):
+                if n_list < 2:
+                    codes, scales = wc_codes[a, b, t]
+                    weights = codes.bitcast(E4M3)
+                    moving_scale = picked_planes[n_list][4 * a : P, js]
+                else:
+                    weights = wn_codes[b][:, a, t, :].bitcast(E2M1)
+                    scales = wn_scale[:, a, b, t, :]
+                    moving_scale = (picked_planes[2], node_plane1)[a][:, js]
+                nc.tensor.matmul_mx(
+                    out=bank[:, cols],
+                    lhsT=weights,
+                    lhsT_scale=scales,
+                    rhs=picked[n_list, a][:, js].bitcast(E4M3),
+                    rhs_scale=moving_scale,
+                    start=(a == 0),
+                    stop=(a == 1),
+                )
+
+        def unit(b, js, width, slots, larger, smaller):
+            banks = [psum.tile([P, BANK], F32, name=nm) for nm in ("first", "second", "node")]
+            for n_list in range(3):
+                for n_slot, t in enumerate(slots):
+                    scores(banks[n_list], slice(n_slot * width, (n_slot + 1) * width), n_list, b, t, js)
+            first = ring.tile([P, BANK], F32, name="first_sb")
+            nc.scalar.copy(out=first[:], in_=banks[0][:])
+            sine = ring.tile([P, BANK], F32, name="sine")
+            for n_slot, t in enumerate(slots):
+                cols = slice(n_slot * width, (n_slot + 1) * width)
+                nc.scalar.activation(out=sine[:, cols], in_=banks[2][:, cols], func=SIN, bias=bias[:, b, RUN * t : RUN * t + 1])
+            mine = slice(slots[0] * width, slots[0] * width + BANK)
+            nc.vector.tensor_tensor(out=larger[:, mine], in0=banks[1][:], in1=first[:], op=ALU.max)
+            nc.vector.tensor_tensor(out=smaller[:, mine], in0=banks[1][:], in1=first[:], op=ALU.min)
+            nc.vector.tensor_tensor(out=larger[:, mine], in0=larger[:, mine], in1=sine[:], op=ALU.mult)
+
+        def finish(larger, smaller, width, name):
+            grouped = ring.tile([P, width, PACK], BF16, name="h_grouped", align_bytes=64)
+            nc.vector.tensor_tensor(
+                out=grouped[:].rearrange("p (c i) t -> p c t i", i=4),
+                in0=larger[:].rearrange("p (t c i) -> p c t i", t=PACK, i=4),
+                in1=smaller[:].rearrange("p (t c i) -> p c t i", t=PACK, i=4),
+                op=ALU.add,
+            )
+            return quantise(grouped[:].rearrange("p c t -> p (c t)"), width, name)
+
+        def project(j0, width, h_low, h_high, last):
+            per_bank = 2 if width == 256 else 3
+            js = slice(j0, j0 + width)
+            halves = ((h_low[0][:, js], h_low[1][:, js]), (h_high[0][:], h_high[1][:]))
+            for n_bank in range(N // P // per_bank):
+                bank = psum.tile([P, per_bank, width], F32, name="result")
+                for b in range(2):
+                    for n_slot in range(per_bank):
+                        codes, scales = wo_codes[b, n_bank * per_bank + n_slot]
+                        nc.tensor.matmul_mx(
+                            out=bank[:, n_slot, :],
+                            lhsT=codes.bitcast(E4M3),
+                            lhsT_scale=scales,
+                            rhs=halves[b][0].bitcast(E4M3),
+                            rhs_scale=halves[b][1],
+                            start=(b == 0 and n_slot == 0),
+                            stop=(b == 1 and n_slot == per_bank - 1),
+                        )
+                staged = ring.tile([P, per_bank, width], F32, name="staged", bufs=3)
+                if last and n_bank == 0:
+                    nc.vector.tensor_copy(out=staged[:], in_=bank[:])
+                else:
+                    nc.scalar.copy(out=staged[:], in_=bank[:])
+                rows = slice(n_bank * per_bank * P, (n_bank + 1) * per_bank * P)
+                nc.sync.dma_start(out=out[rows, js].rearrange("(s p) j -> p s j", p=P), in_=staged[:])
+
+        def chunk_tiles(width, name):
+            larger = keep.tile([P, PACK * width], F32, name="larger" + name)
+            smaller = keep.tile([P, PACK * width], F32, name="smaller" + name)
+            return larger, smaller
+
+        make_wc(0, 0, (0, 1), False)
+        deal_wn(0)
+        make_wc(0, 0, (2, 3), False)
+        make_wc(1, 0, (0,), True)
+        make_wc(1, 0, (1,), True)
+        make_wc(1, 0, (2, 3), False)
+        larger, smaller = chunk_tiles(S, "0")
+        for t in range(PACK):
+            unit(0, slice(0, S), S, (t,), larger, smaller)
+            make_wc(t // 2, 1, ((0, 1), (2, 3))[t % 2], False)
+        deal_wn(1)
+        h_low = finish(larger, smaller, S, "h0")
+
+        wo_parts = [(b, pair) for b in range(2) for pair in range(3)]
+        pending = None
+        for n_chunk, (j0, width) in enumerate(((0, 256), (256, 128), (384, 128))):
+            js = slice(j0, j0 + width)
+            larger, smaller = chunk_tiles(width, "1%d" % n_chunk)
+            per_unit = BANK // width
+            for t0 in range(0, PACK, per_unit):
+                unit(1, js, width, tuple(range(t0, t0 + per_unit)), larger, smaller)
+                for b, pair in wo_parts[:3]:
+                    make_wo(b, pair)
+                wo_parts = wo_parts[3:]
+            if pending is not None:
+                project(*pending, False)
+            pending = (j0, width, h_low, finish(larger, smaller, width, "h1%d" % n_chunk))
+        project(*pending, True)

@@ -33,10 +33,11 @@ def tile_list_modem_parent_features_kernel(
         ring = ctx.enter_context(tc.tile_pool(name="ring", bufs=2))
         psum = ctx.enter_context(tc.psum_pool(name="psum", bufs=2))
 
-        tab_planes = keep.tile([P, T], U8, name="tab_planes", align_bytes=64)
-        nc.vector.memset(tab_planes[:].bitcast(I32), 0)
+        tab_planes = keep.tile([P, T], U8, name="tab_planes", tag="planes_then_words", align_bytes=64)
+        nc.gpsimd.memset(tab_planes[:, 0 : T // 2].bitcast(I32), 0)
+        nc.vector.memset(tab_planes[:, T // 2 : T].bitcast(I32), 0)
         for q in range(4):
-            nc.scalar.dma_start(
+            nc.sync.dma_start(
                 out=tab_planes[32 * q : 32 * q + 8, :].bitcast(I32),
                 in_=tab_scales[:, 4 * q : 4 * q + 4, :].bitcast(I32),
             )
@@ -46,26 +47,22 @@ def tile_list_modem_parent_features_kernel(
             nc.sync.dma_start(tile[:], source)
             lists.append(tile)
 
+        wn_planes = keep.tile([P, 2, H], U8, name="wn_planes", align_bytes=64)
+        nc.vector.memset(wn_planes[:].rearrange("p a c -> p (a c)").bitcast(I32), 0)
+        node_plane1 = keep.tile([P, S], U8, name="node_plane1", align_bytes=64)
+        nc.vector.memset(node_plane1[:].bitcast(I32), 0)
         bias = keep.tile([P, 2, 16], F32, name="bias")
         bn_runs = bn.rearrange("(b u x) -> u b x", b=2, x=16)
         for i in range(RUN):
-            nc.sync.dma_start(out=bias[i:P:RUN, :, 0:13], in_=bn_runs[:, :, i : i + 13])
+            nc.gpsimd.dma_start(out=bias[i:P:RUN, :, 0:13], in_=bn_runs[:, :, i : i + 13])
 
-        wn_planes = keep.tile([P, 2, H], U8, name="wn_planes", align_bytes=64)
-        nc.gpsimd.memset(wn_planes[:].rearrange("p a c -> p (a c)").bitcast(I32), 0)
-        for q in range(4):
-            nc.gpsimd.dma_start(
-                out=wn_planes[32 * q : 32 * q + 4, :, :].bitcast(I32),
-                in_=wn_scales[:, 4 * q : 4 * q + 4, :].rearrange("a q c -> q a c").bitcast(I32),
-            )
-        node_plane1 = keep.tile([P, S], U8, name="node_plane1", align_bytes=64)
-        nc.gpsimd.memset(node_plane1[:].bitcast(I32), 0)
+        table = {}
 
-        table = []
-        for a in range(2):
+        def load_table(a):
             tile = keep.tile([P, T], I32, name="table%d" % a, align_bytes=64)
             nc.sync.dma_start(out=tile[:], in_=tab_words[a].rearrange("p t i -> p (t i)").bitcast(I32))
-            table.append(tile)
+            table[a] = tile
+
         wc_raw = {}
         wn_raw = {}
         wo_raw = {}
@@ -93,36 +90,47 @@ def tile_list_modem_parent_features_kernel(
                 nc.sync.dma_start(out=tile[:, t, :], in_=rows[t])
             wo_raw[b] = tile
 
-        for b in range(2):
-            load_wc(0, b)
-            load_wn(b)
-            load_wc(1, b)
+        load_table(0)
+        load_wn(0)
+        load_table(1)
+        for q in range(4):
+            nc.sync.dma_start(
+                out=wn_planes[32 * q : 32 * q + 4, :, :].bitcast(I32),
+                in_=wn_scales[:, 4 * q : 4 * q + 4, :].rearrange("a q c -> q a c").bitcast(I32),
+            )
+        load_wc(0, 0)
+        load_wc(1, 0)
+        load_wc(0, 1)
+        load_wn(1)
+        load_wc(1, 1)
         for b in range(2):
             load_wo(b)
 
+        picked = {}
+
+        def pick_words(a):
+            tile = keep.tile(
+                [P, 3, S], U32, name="picked%d" % a, tag=("words0", "planes_then_words")[a], align_bytes=64
+            )
+            for n_list in range(3):
+                nc.vector.tensor_copy(out=tile[:, n_list, :], in_=table[a][:].bitcast(U32).indirect(lists[n_list][:]))
+                picked[n_list, a] = tile[:, n_list, :]
+
+        pick_words(0)
         picked_planes = {}
         for n_list in (2, 0, 1):
             tile = keep.tile([P, S], U8, name="picked_planes%d" % n_list, align_bytes=64)
             nc.vector.tensor_copy(out=tile[:], in_=tab_planes[:].indirect(lists[n_list][:]))
             picked_planes[n_list] = tile
-        nc.gpsimd.dma_start(
+        nc.scalar.dma_start(
             out=node_plane1[0 : P - 4, :].bitcast(I32), in_=picked_planes[2][4:P, :].bitcast(I32)
         )
-        picked = {}
-
-        def pick_words(a):
-            for n_list in range(3):
-                tile = keep.tile([P, S], U32, name="picked%d%d" % (n_list, a), align_bytes=64)
-                nc.vector.tensor_copy(out=tile[:], in_=table[a][:].bitcast(U32).indirect(lists[n_list][:]))
-                picked[n_list, a] = tile
-
-        pick_words(0)
+        pick_words(1)
         wn_scale = keep.tile([P, 2, 2, PACK, P], U8, name="wn_scale", align_bytes=64)
         nc.vector.tensor_copy(
             out=wn_scale[:].bitcast(I32).rearrange("p a b t u -> p (a b) t u"),
             in_=wn_planes[:].bitcast(I32).rearrange("p a (b u t) -> p (a b) t u", b=2, t=PACK),
         )
-        pick_words(1)
 
         wn_codes = {}
 

@@ -37,51 +37,45 @@ def tile_list_modem_parent_features_kernel(
         nc.gpsimd.memset(tab_planes[:, 0 : T // 2].bitcast(I32), 0)
         nc.vector.memset(tab_planes[:, T // 2 : T].bitcast(I32), 0)
         for q in range(4):
-            nc.sync.dma_start(
-                out=tab_planes[32 * q : 32 * q + 8, :].bitcast(I32),
-                in_=tab_scales[:, 4 * q : 4 * q + 4, :].bitcast(I32),
-            )
-        lists = []
-        for n_list, source in enumerate((offs, offs2, offs3)):
+            for a in range(2):
+                nc.sync.dma_start(
+                    out=tab_planes[32 * q + 4 * a : 32 * q + 4 * a + 4, :].bitcast(I32),
+                    in_=tab_scales[a, 4 * q : 4 * q + 4, :].bitcast(I32),
+                )
+        warm = keep.tile([P, 2], F32, name="warm")
+        nc.vector.memset(warm[:], 0.0)
+        nc.scalar.activation(out=warm[:, 1:2], in_=warm[:, 0:1], func=SIN)
+        lists = {}
+        for n_list in (2, 0, 1):
             tile = lists_pool.tile([P, S // 16], U16, name="list%d" % n_list)
-            nc.sync.dma_start(tile[:], source)
-            lists.append(tile)
+            nc.sync.dma_start(tile[:], (offs, offs2, offs3)[n_list])
+            lists[n_list] = tile
 
         wn_planes = keep.tile([P, 2, H], U8, name="wn_planes", align_bytes=64)
         nc.vector.memset(wn_planes[:].rearrange("p a c -> p (a c)").bitcast(I32), 0)
         node_plane1 = keep.tile([P, S], U8, name="node_plane1", align_bytes=64)
         nc.vector.memset(node_plane1[:].bitcast(I32), 0)
-        bias = keep.tile([P, 2, 16], F32, name="bias")
-        bn_runs = bn.rearrange("(b u x) -> u b x", b=2, x=16)
-        for i in range(RUN):
-            nc.gpsimd.dma_start(out=bias[i:P:RUN, :, 0:13], in_=bn_runs[:, :, i : i + 13])
 
         table = {}
+        wc_raw = {}
+        wo_raw = {}
+        shared = keep.tile([P, 2 * S + PACK * KP], F32, name="shared", align_bytes=64)
 
         def load_table(a):
             tile = keep.tile([P, T], I32, name="table%d" % a, align_bytes=64)
             nc.sync.dma_start(out=tile[:], in_=tab_words[a].rearrange("p t i -> p (t i)").bitcast(I32))
             table[a] = tile
 
-        wc_raw = {}
-        wn_raw = {}
-        wo_raw = {}
-
         def load_wc(a, b):
-            tile = keep.tile([P, PACK, KP], F32, name="wc_raw%d%d" % (a, b))
+            if (a, b) == (0, 1):
+                raw = shared[:, 2 * S :].rearrange("p (j c) -> p j c", j=PACK)
+            else:
+                raw = keep.tile([P, PACK, KP], F32, name="wc_raw%d%d" % (a, b))[:]
             nc.sync.dma_start(
-                out=tile[:],
+                out=raw,
                 in_=wc[a * KP : (a + 1) * KP, b * KP : (b + 1) * KP].rearrange("(p j) c -> p j c", j=PACK),
             )
-            wc_raw[a, b] = tile
-
-        def load_wn(b):
-            tile = keep.tile([P, 2, KP // 2], I32, name="wn_raw%d" % b)
-            nc.sync.dma_start(
-                out=tile[:],
-                in_=wn_words[:, :, 2 * b * KP : 2 * (b + 1) * KP].rearrange("a p c -> p a c").bitcast(I32),
-            )
-            wn_raw[b] = tile
+            wc_raw[a, b] = raw
 
         def load_wo(b):
             tile = keep.tile([P, PACK, N], F32, name="wo_raw%d" % b)
@@ -90,152 +84,152 @@ def tile_list_modem_parent_features_kernel(
                 nc.sync.dma_start(out=tile[:, t, :], in_=rows[t])
             wo_raw[b] = tile
 
-        load_table(0)
-        load_wn(0)
-        load_table(1)
         for q in range(4):
             nc.sync.dma_start(
                 out=wn_planes[32 * q : 32 * q + 4, :, :].bitcast(I32),
                 in_=wn_scales[:, 4 * q : 4 * q + 4, :].rearrange("a q c -> q a c").bitcast(I32),
             )
-        load_wc(0, 0)
-        load_wc(1, 0)
-        load_wc(0, 1)
-        load_wn(1)
-        load_wc(1, 1)
-        for b in range(2):
-            load_wo(b)
+        load_table(0)
+        wn_raw = keep.tile([P, 2, H // 2], I32, name="wn_raw")
+        nc.sync.dma_start(out=wn_raw[:], in_=wn_words.rearrange("a p c -> p a c").bitcast(I32))
+        load_table(1)
+        bias = keep.tile([P, 2, 16], F32, name="bias")
+        bn_runs = bn.rearrange("(b u x) -> u b x", b=2, x=16)
+        for i in range(RUN):
+            nc.gpsimd.dma_start(out=bias[i:P:RUN, :, 0:13], in_=bn_runs[:, :, i : i + 13])
 
-        picked = {}
-
-        def pick_words(a):
-            tile = keep.tile(
-                [P, 3, S], U32, name="picked%d" % a, tag=("words0", "planes_then_words")[a], align_bytes=64
-            )
-            for n_list in range(3):
-                nc.vector.tensor_copy(out=tile[:, n_list, :], in_=table[a][:].bitcast(U32).indirect(lists[n_list][:]))
-                picked[n_list, a] = tile[:, n_list, :]
-
-        pick_words(0)
         picked_planes = {}
         for n_list in (2, 0, 1):
             tile = keep.tile([P, S], U8, name="picked_planes%d" % n_list, align_bytes=64)
             nc.vector.tensor_copy(out=tile[:], in_=tab_planes[:].indirect(lists[n_list][:]))
             picked_planes[n_list] = tile
-        nc.scalar.dma_start(
-            out=node_plane1[0 : P - 4, :].bitcast(I32), in_=picked_planes[2][4:P, :].bitcast(I32)
+        for p0, p1 in ((0, 64), (64, 100)):
+            nc.sync.dma_start(
+                out=node_plane1[p0:p1, :].bitcast(I32), in_=picked_planes[2][p0 + 4 : p1 + 4, :].bitcast(I32)
+            )
+        for b in range(2):
+            for a in range(2):
+                load_wc(a, b)
+        for b in range(2):
+            load_wo(b)
+        picked = {}
+
+        def pick_words(a, n_list, target):
+            nc.vector.tensor_copy(out=target, in_=table[a][:].bitcast(U32).indirect(lists[n_list][:]))
+            picked[n_list, a] = target
+
+        words_low = keep.tile([P, 3, S], U32, name="words_low", tag="planes_then_words", align_bytes=64)
+        for n_list in (2, 0, 1):
+            pick_words(0, n_list, words_low[:, n_list, :])
+        wn_codes = keep.tile([P, 2, 2, PACK, 2 * P], U8, name="wn_codes", align_bytes=64)
+        nc.vector.tensor_copy(
+            out=wn_codes[:].bitcast(I32).rearrange("p a b t (u w) -> p (a b) t u w", w=2),
+            in_=wn_raw[:].rearrange("p a (b u t w) -> p (a b) t u w", b=2, t=PACK, w=2),
         )
-        pick_words(1)
         wn_scale = keep.tile([P, 2, 2, PACK, P], U8, name="wn_scale", align_bytes=64)
         nc.vector.tensor_copy(
             out=wn_scale[:].bitcast(I32).rearrange("p a b t u -> p (a b) t u"),
             in_=wn_planes[:].bitcast(I32).rearrange("p a (b u t) -> p (a b) t u", b=2, t=PACK),
         )
+        for n_list in (2, 0, 1):
+            tile = keep.tile([P, S], U32, name="words_high%d" % n_list, align_bytes=64)
+            pick_words(1, n_list, tile[:])
 
-        wn_codes = {}
+        sine = {}
 
-        def deal_wn(b):
-            tile = keep.tile([P, 2, PACK, 2 * P], U8, name="wn_codes%d" % b, align_bytes=64)
-            nc.vector.tensor_copy(
-                out=tile[:].bitcast(I32).rearrange("p a t (u w) -> p a t u w", w=2),
-                in_=wn_raw[b][:].rearrange("p a (u t w) -> p a t u w", t=PACK, w=2),
-            )
-            wn_codes[b] = tile
+        def make_sines(b, tile):
+            for t in range(PACK):
+                bank = psum.tile([P, BANK], F32, name="node")
+                for a in range(2):
+                    nc.tensor.matmul_mx(
+                        out=bank[:],
+                        lhsT=wn_codes[:, a, b, t, :].bitcast(E2M1),
+                        lhsT_scale=wn_scale[:, a, b, t, :],
+                        rhs=picked[2, a].bitcast(E4M3),
+                        rhs_scale=(picked_planes[2], node_plane1)[a][:],
+                        start=(a == 0),
+                        stop=(a == 1),
+                    )
+                nc.scalar.activation(
+                    out=tile[:, t * S : (t + 1) * S], in_=bank[:], func=SIN, bias=bias[:, b, RUN * t : RUN * t + 1]
+                )
+            sine[b] = tile
 
-        wc_codes = {}
+        make_sines(0, keep.tile([P, PACK * S], F32, name="sine0", align_bytes=64)[:])
 
-        def round_wc(a, b, t, grouped, on_vector):
-            src_ap = wc_raw[a, b][:].rearrange("p j (u t i) -> p t u j i", t=PACK, i=RUN)[:, t]
-            dst_ap = grouped.rearrange("p (u i) j -> p u j i", i=RUN)
-            if on_vector:
-                nc.vector.tensor_copy(out=dst_ap, in_=src_ap)
-            else:
-                nc.scalar.copy(out=dst_ap, in_=src_ap)
-
-        def quantise(grouped, width, name):
+        def quantise(grouped, name):
+            width = grouped.shape[1] // PACK
             codes = keep.tile([P, width], U32, name=name + "_codes", align_bytes=64)
             scales = keep.tile([P, width], U8, name=name + "_scales", align_bytes=64)
             nc.vector.quantize_mx(out=codes[:].bitcast(E4M3), scales=scales[:], in_=grouped)
             return codes, scales
 
-        def make_wc(a, b, slots, on_vector):
-            grouped = ring.tile([P, len(slots), P, PACK], BF16, name="wc_grouped", tag="grouped", bufs=4, align_bytes=64)
-            for n_slot, t in enumerate(slots):
-                round_wc(a, b, t, grouped[:, n_slot], on_vector)
-            codes, scales = quantise(
-                grouped[:].rearrange("p s m j -> p (s m j)"), len(slots) * P, "wc%d%d%d" % (a, b, slots[0])
-            )
-            for n_slot, t in enumerate(slots):
-                cols = slice(n_slot * P, (n_slot + 1) * P)
-                wc_codes[a, b, t] = (codes[:, cols], scales[:, cols])
-
+        wc_codes = {}
         wo_codes = {}
 
-        def make_wo(b, pair):
-            grouped = ring.tile([P, 2, P, PACK], BF16, name="wo_grouped", tag="grouped", bufs=4, align_bytes=64)
-            for half in range(2):
-                n0 = (2 * pair + half) * P
-                nc.scalar.copy(
-                    out=grouped[:, half].rearrange("p (c i) t -> p c t i", i=4),
-                    in_=wo_raw[b][:, :, n0 : n0 + P].rearrange("p t (c i) -> p c t i", i=4),
-                )
-            codes, scales = quantise(grouped[:].rearrange("p s m j -> p (s m j)"), 2 * P, "wo%d%d" % (b, pair))
-            for half in range(2):
-                cols = slice(half * P, (half + 1) * P)
-                wo_codes[b, 2 * pair + half] = (codes[:, cols], scales[:, cols])
+        def round_wc(copy, a, b, t0, n_slots, grouped):
+            copy(
+                out=grouped.rearrange("p (t u i j) -> p t u j i", t=n_slots, i=RUN, j=PACK),
+                in_=wc_raw[a, b].rearrange("p j (u t i) -> p t u j i", t=PACK, i=RUN)[:, t0 : t0 + n_slots],
+            )
 
-        def scores(bank, cols, n_list, b, t, js):
-            for a in range(2):
-                if n_list < 2:
-                    codes, scales = wc_codes[a, b, t]
-                    weights = codes.bitcast(E4M3)
-                    moving_scale = picked_planes[n_list][4 * a : P, js]
-                else:
-                    weights = wn_codes[b][:, a, t, :].bitcast(E2M1)
-                    scales = wn_scale[:, a, b, t, :]
-                    moving_scale = (picked_planes[2], node_plane1)[a][:, js]
-                nc.tensor.matmul_mx(
-                    out=bank[:, cols],
-                    lhsT=weights,
-                    lhsT_scale=scales,
-                    rhs=picked[n_list, a][:, js].bitcast(E4M3),
-                    rhs_scale=moving_scale,
-                    start=(a == 0),
-                    stop=(a == 1),
-                )
+        def quantise_tiles(book, key, first_tile, grouped):
+            codes, scales = quantise(grouped, "q%s_%d" % ("".join(str(x) for x in key), first_tile))
+            for n_tile in range(grouped.shape[1] // KP):
+                cols = slice(n_tile * P, (n_tile + 1) * P)
+                book[key[1:] + (first_tile + n_tile,)] = (codes[:, cols], scales[:, cols])
 
-        def unit(b, js, width, slots, larger, smaller):
-            banks = [psum.tile([P, BANK], F32, name=nm) for nm in ("first", "second", "node")]
-            for n_list in range(3):
+        def round_wo(b, pair, grouped):
+            n0 = 2 * P * pair
+            nc.scalar.copy(
+                out=grouped.rearrange("p (c i t) -> p c t i", i=4, t=PACK),
+                in_=wo_raw[b][:, :, n0 : n0 + 2 * P].rearrange("p t (c i) -> p c t i", i=4),
+            )
+
+        def products(b, js, slots, first):
+            width = BANK // len(slots)
+            banks = [psum.tile([P, BANK], F32, name=nm) for nm in ("first", "second")]
+            for n_list in range(2):
                 for n_slot, t in enumerate(slots):
-                    scores(banks[n_list], slice(n_slot * width, (n_slot + 1) * width), n_list, b, t, js)
-            first = ring.tile([P, BANK], F32, name="first_sb")
-            nc.scalar.copy(out=first[:], in_=banks[0][:])
-            sine = ring.tile([P, BANK], F32, name="sine")
-            for n_slot, t in enumerate(slots):
-                cols = slice(n_slot * width, (n_slot + 1) * width)
-                nc.scalar.activation(out=sine[:, cols], in_=banks[2][:, cols], func=SIN, bias=bias[:, b, RUN * t : RUN * t + 1])
-            mine = slice(slots[0] * width, slots[0] * width + BANK)
-            nc.vector.tensor_tensor(out=larger[:, mine], in0=banks[1][:], in1=first[:], op=ALU.max)
-            nc.vector.tensor_tensor(out=smaller[:, mine], in0=banks[1][:], in1=first[:], op=ALU.min)
-            nc.vector.tensor_tensor(out=larger[:, mine], in0=larger[:, mine], in1=sine[:], op=ALU.mult)
+                    for a in range(2):
+                        codes, scales = wc_codes[a, b, t]
+                        nc.tensor.matmul_mx(
+                            out=banks[n_list][:, n_slot * width : (n_slot + 1) * width],
+                            lhsT=codes.bitcast(E4M3),
+                            lhsT_scale=scales,
+                            rhs=picked[n_list, a][:, js].bitcast(E4M3),
+                            rhs_scale=picked_planes[n_list][4 * a : P, js],
+                            start=(a == 0),
+                            stop=(a == 1),
+                        )
+            nc.scalar.copy(out=first, in_=banks[0][:])
+            return banks[1], first
 
-        def finish(larger, smaller, width, name):
-            grouped = ring.tile([P, width, PACK], BF16, name="h_grouped", align_bytes=64)
+        def take(op, target, n_unit, made):
+            mine = slice(n_unit * BANK, (n_unit + 1) * BANK)
+            nc.vector.tensor_tensor(out=target[:, mine], in0=made[0][:], in1=made[1], op=op)
+
+        def turn(engine, larger, n_unit, b, js, slots):
+            mine = larger[:, n_unit * BANK : (n_unit + 1) * BANK].rearrange("p (t j) -> p t j", t=len(slots))
+            factor = sine[b].rearrange("p (t j) -> p t j", t=PACK)[:, slots[0] : slots[-1] + 1, js]
+            engine.tensor_tensor(out=mine, in0=mine, in1=factor, op=ALU.mult)
+
+        def join(larger, smaller, width):
+            grouped = keep.tile([P, PACK * width], BF16, name="h_grouped", tag="h%d" % smaller.shape[1], bufs=1 if width > P else 2, align_bytes=64)
             nc.vector.tensor_tensor(
-                out=grouped[:].rearrange("p (c i) t -> p c t i", i=4),
-                in0=larger[:].rearrange("p (t c i) -> p c t i", t=PACK, i=4),
-                in1=smaller[:].rearrange("p (t c i) -> p c t i", t=PACK, i=4),
+                out=grouped[:].rearrange("p (c i t) -> p c t i", i=2, t=PACK),
+                in0=larger[:, 0 : PACK * width].rearrange("p (t c i) -> p c t i", t=PACK, i=2),
+                in1=smaller[:].rearrange("p (t c i) -> p c t i", t=PACK, i=2),
                 op=ALU.add,
             )
-            return quantise(grouped[:].rearrange("p c t -> p (c t)"), width, name)
+            return grouped
 
         def project(j0, width, h_low, h_high, last):
             per_bank = 2 if width == 256 else 3
             js = slice(j0, j0 + width)
             halves = ((h_low[0][:, js], h_low[1][:, js]), (h_high[0][:], h_high[1][:]))
             for n_bank in range(N // P // per_bank):
-                bank = psum.tile([P, per_bank, width], F32, name="result")
+                bank = psum.tile([P, per_bank, width], F32, name="result", tag="node" if last else "result")
                 for b in range(2):
                     for n_slot in range(per_bank):
                         codes, scales = wo_codes[b, n_bank * per_bank + n_slot]
@@ -248,7 +242,7 @@ def tile_list_modem_parent_features_kernel(
                             start=(b == 0 and n_slot == 0),
                             stop=(b == 1 and n_slot == per_bank - 1),
                         )
-                staged = ring.tile([P, per_bank, width], F32, name="staged", bufs=3)
+                staged = ring.tile([P, per_bank, width], F32, name="staged", bufs=7)
                 if last and n_bank == 0:
                     nc.vector.tensor_copy(out=staged[:], in_=bank[:])
                 else:
@@ -256,36 +250,84 @@ def tile_list_modem_parent_features_kernel(
                 rows = slice(n_bank * per_bank * P, (n_bank + 1) * per_bank * P)
                 nc.sync.dma_start(out=out[rows, js].rearrange("(s p) j -> p s j", p=P), in_=staged[:])
 
-        def chunk_tiles(width, name):
-            larger = keep.tile([P, PACK * width], F32, name="larger" + name)
-            smaller = keep.tile([P, PACK * width], F32, name="smaller" + name)
-            return larger, smaller
+        all_slots = tuple(range(PACK))
+        whole = slice(0, S)
 
-        make_wc(0, 0, (0, 1), False)
-        deal_wn(0)
-        make_wc(0, 0, (2, 3), False)
-        make_wc(1, 0, (0,), True)
-        make_wc(1, 0, (1,), True)
-        make_wc(1, 0, (2, 3), False)
-        larger, smaller = chunk_tiles(S, "0")
+        early = keep.tile([P, 2, PACK * KP], BF16, name="early", tag="table1", align_bytes=64)
+
+        def early_part(a, t0, n_slots):
+            return early[:, a, t0 * KP : (t0 + n_slots) * KP]
+
+        round_wc(nc.scalar.copy, 0, 0, 2, 2, early_part(0, 2, 2))
+        round_wc(nc.vector.tensor_copy, 0, 0, 0, 2, early_part(0, 0, 2))
+        round_wc(nc.vector.tensor_copy, 1, 0, 0, 1, early_part(1, 0, 1))
+        quantise_tiles(wc_codes, ("c", 0, 0), 0, early_part(0, 0, 2))
+        quantise_tiles(wc_codes, ("c", 1, 0), 0, early_part(1, 0, 1))
+        round_wc(nc.vector.tensor_copy, 1, 0, 1, 1, early_part(1, 1, 1))
+        round_wc(nc.vector.tensor_copy, 1, 0, 2, 2, early_part(1, 2, 2))
+        quantise_tiles(wc_codes, ("c", 1, 0), 1, early_part(1, 1, 1))
+        quantise_tiles(wc_codes, ("c", 0, 0), 2, early_part(0, 2, 2))
+        quantise_tiles(wc_codes, ("c", 1, 0), 2, early_part(1, 2, 2))
+
+        firsts = [keep.tile([P, 2 * BANK], F32, name="first%d" % n, align_bytes=64) for n in range(4)]
+
+        def first_of(n_unit):
+            return firsts[n_unit // 2][:, (n_unit % 2) * BANK : (n_unit % 2 + 1) * BANK]
+
+        larger = keep.tile([P, PACK * S], F32, name="larger")
+        smaller = keep.tile([P, PACK * S], F32, name="smaller0")
         for t in range(PACK):
-            unit(0, slice(0, S), S, (t,), larger, smaller)
-            make_wc(t // 2, 1, ((0, 1), (2, 3))[t % 2], False)
-        deal_wn(1)
-        h_low = finish(larger, smaller, S, "h0")
+            made = products(0, whole, (t,), first_of(t))
+            take(ALU.max, larger, t, made)
+            take(ALU.min, smaller, t, made)
+            turn(nc.gpsimd if t < 3 else nc.vector, larger, t, 0, whole, (t,))
+            copy = nc.scalar.copy if t < 3 else nc.vector.tensor_copy
+            round_wc(copy, t // 2, 1, 2 * (t % 2), 2, first_of(t).bitcast(BF16))
+        make_sines(1, shared[:, 0 : PACK * S])
+        for a in range(2):
+            quantise_tiles(wc_codes, ("c", a, 1), 0, firsts[a][:].bitcast(BF16))
+        grouped_low = join(larger, smaller, S)
 
-        wo_parts = [(b, pair) for b in range(2) for pair in range(3)]
-        pending = None
-        for n_chunk, (j0, width) in enumerate(((0, 256), (256, 128), (384, 128))):
-            js = slice(j0, j0 + width)
-            larger, smaller = chunk_tiles(width, "1%d" % n_chunk)
-            per_unit = BANK // width
-            for t0 in range(0, PACK, per_unit):
-                unit(1, js, width, tuple(range(t0, t0 + per_unit)), larger, smaller)
-                for b, pair in wo_parts[:3]:
-                    make_wo(b, pair)
-                wo_parts = wo_parts[3:]
-            if pending is not None:
-                project(*pending, False)
-            pending = (j0, width, h_low, finish(larger, smaller, width, "h1%d" % n_chunk))
-        project(*pending, True)
+        wide = slice(0, 256)
+        mid = slice(256, 384)
+        end = slice(384, 512)
+        smaller = keep.tile([P, PACK * 256], F32, name="smaller1")
+        smaller_mid = keep.tile([P, BANK], F32, name="smaller_mid")
+        smaller_end = keep.tile([P, BANK], F32, name="smaller_end")
+        larger_end = keep.tile([P, BANK], F32, name="larger_end")
+        made = products(1, wide, (0, 1), first_of(4))
+        take(ALU.min, smaller, 0, made)
+        h_low = quantise(grouped_low[:], "h0")
+        take(ALU.max, larger, 0, made)
+        turn(nc.gpsimd, larger, 0, 1, wide, (0, 1))
+        made = products(1, wide, (2, 3), first_of(5))
+        take(ALU.max, larger, 1, made)
+        take(ALU.min, smaller, 1, made)
+        made_mid = products(1, mid, all_slots, first_of(6))
+        made_end = products(1, end, all_slots, first_of(7))
+        wo_low = sine[0].bitcast(BF16)
+        for pair in range(3):
+            round_wo(0, pair, wo_low[:, pair * 2 * KP : (pair + 1) * 2 * KP])
+        wo_high = [grouped_low[:, 0 : 2 * KP], grouped_low[:, 2 * KP : 4 * KP], first_of(4).bitcast(BF16)]
+        for pair in range(3):
+            round_wo(1, pair, wo_high[pair])
+        turn(nc.vector, larger, 1, 1, wide, (2, 3))
+        take(ALU.min, smaller_mid, 0, made_mid)
+        grouped = join(larger, smaller, 256)
+        quantise_tiles(wo_codes, ("o", 0), 0, wo_low[:, 0 : 4 * KP])
+        quantise_tiles(wo_codes, ("o", 0), 4, wo_low[:, 4 * KP : 6 * KP])
+        h_wide = quantise(grouped[:], "h_wide")
+        quantise_tiles(wo_codes, ("o", 1), 0, grouped_low[:])
+        quantise_tiles(wo_codes, ("o", 1), 4, wo_high[2])
+        project(0, 256, h_low, h_wide, False)
+        take(ALU.max, larger, 0, made_mid)
+        turn(nc.gpsimd, larger, 0, 1, mid, all_slots)
+        take(ALU.max, larger_end, 0, made_end)
+        take(ALU.min, smaller_end, 0, made_end)
+        grouped = join(larger, smaller_mid, P)
+        turn(nc.vector, larger_end, 0, 1, end, all_slots)
+        h_mid = quantise(grouped[:], "h_mid")
+        project(mid.start, P, h_low, h_mid, False)
+        grouped_end = join(larger_end, smaller_end, P)
+        h_end = quantise(grouped_end[:], "h_end")
+        project(end.start, P, h_low, h_end, True)

from contextlib import ExitStack

import concourse.mybir as mybir

K, T, S, H, N = 1024, 4096, 512, 1024, 768
FLOPS = 2 * S * (3 * K * H + H * N)

F32 = mybir.dt.float32
BF16 = mybir.dt.bfloat16
I32 = mybir.dt.int32
U32 = mybir.dt.uint32
U16 = mybir.dt.uint16
U8 = mybir.dt.uint8
E4M3 = mybir.dt.float8_e4m3fn_x4
E2M1 = mybir.dt.float4_e2m1fn_x4
ALU = mybir.AluOpType
SIN = mybir.ActivationFunctionType.Sin

P = 128
PACK = 4
KP = P * PACK
BANK = 512
RUN = 4


def tile_list_modem_parent_features_kernel(
    tc, tab_words, tab_scales, offs, offs2, offs3, wc, wn_words, wn_scales, bn, wo, out
):
    nc = tc.nc
    with ExitStack() as ctx:
        lists_pool = ctx.enter_context(tc.tile_pool(name="lists", bufs=1))
        keep = ctx.enter_context(tc.tile_pool(name="keep", bufs=1))
        ring = ctx.enter_context(tc.tile_pool(name="ring", bufs=2))
        psum = ctx.enter_context(tc.psum_pool(name="psum", bufs=2))

        tab_planes = keep.tile([P, T], U8, name="tab_planes", tag="planes_then_words", align_bytes=64)
        nc.gpsimd.memset(tab_planes[:, 0 : T // 2].bitcast(I32), 0)
        nc.vector.memset(tab_planes[:, T // 2 : T].bitcast(I32), 0)
        for q in range(4):
            for a in range(2):
                nc.sync.dma_start(
                    out=tab_planes[32 * q + 4 * a : 32 * q + 4 * a + 4, :].bitcast(I32),
                    in_=tab_scales[a, 4 * q : 4 * q + 4, :].bitcast(I32),
                )
        warm = keep.tile([P, 2], F32, name="warm")
        nc.vector.memset(warm[:], 0.0)
        nc.scalar.activation(out=warm[:, 1:2], in_=warm[:, 0:1], func=SIN)
        lists = {}
        for n_list in (2, 0, 1):
            tile = lists_pool.tile([P, S // 16], U16, name="list%d" % n_list)
            nc.sync.dma_start(tile[:], (offs, offs2, offs3)[n_list])
            lists[n_list] = tile

        wn_planes = keep.tile([P, 2, H], U8, name="wn_planes", align_bytes=64)
        nc.vector.memset(wn_planes[:].rearrange("p a c -> p (a c)").bitcast(I32), 0)
        node_plane1 = keep.tile([P, S], U8, name="node_plane1", align_bytes=64)
        nc.vector.memset(node_plane1[:].bitcast(I32), 0)

        table = {}
        wc_raw = {}
        wo_raw = {}
        shared = keep.tile([P, 2 * S + PACK * KP], F32, name="shared", align_bytes=64)

        def load_table(a):
            tile = keep.tile([P, T], I32, name="table%d" % a, align_bytes=64)
            nc.sync.dma_start(out=tile[:], in_=tab_words[a].rearrange("p t i -> p (t i)").bitcast(I32))
            table[a] = tile

        def load_wc(a, b):
            if (a, b) == (0, 1):
                raw = shared[:, 2 * S :].rearrange("p (j c) -> p j c", j=PACK)
            else:
                raw = keep.tile([P, PACK, KP], F32, name="wc_raw%d%d" % (a, b))[:]
            nc.sync.dma_start(
                out=raw,
                in_=wc[a * KP : (a + 1) * KP, b * KP : (b + 1) * KP].rearrange("(p j) c -> p j c", j=PACK),
            )
            wc_raw[a, b] = raw

        def load_wo(b):
            tile = keep.tile([P, PACK, N], F32, name="wo_raw%d" % b)
            rows = wo[b * KP : (b + 1) * KP, :].rearrange("(u t i) n -> t u i n", t=PACK, i=RUN)
            for t in range(PACK):
                nc.sync.dma_start(out=tile[:, t, :], in_=rows[t])
            wo_raw[b] = tile

        for q in range(4):
            nc.sync.dma_start(
                out=wn_planes[32 * q : 32 * q + 4, :, :].bitcast(I32),
                in_=wn_scales[:, 4 * q : 4 * q + 4, :].rearrange("a q c -> q a c").bitcast(I32),
            )
        load_table(0)
        wn_raw = keep.tile([P, 2, H // 2], I32, name="wn_raw")
        nc.sync.dma_start(out=wn_raw[:], in_=wn_words.rearrange("a p c -> p a c").bitcast(I32))
        load_table(1)
        bias = keep.tile([P, 2, 16], F32, name="bias")
        bn_runs = bn.rearrange("(b u x) -> u b x", b=2, x=16)
        for i in range(RUN):
            nc.gpsimd.dma_start(out=bias[i:P:RUN, :, 0:13], in_=bn_runs[:, :, i : i + 13])

        picked_planes = {}
        for n_list in (2, 0, 1):
            tile = keep.tile([P, S], U8, name="picked_planes%d" % n_list, align_bytes=64)
            nc.vector.tensor_copy(out=tile[:], in_=tab_planes[:].indirect(lists[n_list][:]))
            picked_planes[n_list] = tile
        for p0, p1 in ((0, 64), (64, 100)):
            nc.sync.dma_start(
                out=node_plane1[p0:p1, :].bitcast(I32), in_=picked_planes[2][p0 + 4 : p1 + 4, :].bitcast(I32)
            )
        for b in range(2):
            for a in range(2):
                load_wc(a, b)
        for b in range(2):
            load_wo(b)
        picked = {}

        def pick_words(a, n_list, target):
            nc.vector.tensor_copy(out=target, in_=table[a][:].bitcast(U32).indirect(lists[n_list][:]))
            picked[n_list, a] = target

        words_low = keep.tile([P, 3, S], U32, name="words_low", tag="planes_then_words", align_bytes=64)
        for n_list in (2, 0, 1):
            pick_words(0, n_list, words_low[:, n_list, :])
        wn_codes = keep.tile([P, 2, 2, PACK, 2 * P], U8, name="wn_codes", align_bytes=64)
        nc.vector.tensor_copy(
            out=wn_codes[:].bitcast(I32).rearrange("p a b t (u w) -> p (a b) t u w", w=2),
            in_=wn_raw[:].rearrange("p a (b u t w) -> p (a b) t u w", b=2, t=PACK, w=2),
        )
        wn_scale = keep.tile([P, 2, 2, PACK, P], U8, name="wn_scale", align_bytes=64)
        nc.vector.tensor_copy(
            out=wn_scale[:].bitcast(I32).rearrange("p a b t u -> p (a b) t u"),
            in_=wn_planes[:].bitcast(I32).rearrange("p a (b u t) -> p (a b) t u", b=2, t=PACK),
        )
        for n_list in (2, 0, 1):
            tile = keep.tile([P, S], U32, name="words_high%d" % n_list, align_bytes=64)
            pick_words(1, n_list, tile[:])

        sine = {}

        def make_sines(b, tile):
            for t in range(PACK):
                bank = psum.tile([P, BANK], F32, name="node")
                for a in range(2):
                    nc.tensor.matmul_mx(
                        out=bank[:],
                        lhsT=wn_codes[:, a, b, t, :].bitcast(E2M1),
                        lhsT_scale=wn_scale[:, a, b, t, :],
                        rhs=picked[2, a].bitcast(E4M3),
                        rhs_scale=(picked_planes[2], node_plane1)[a][:],
                        start=(a == 0),
                        stop=(a == 1),
                    )
                nc.scalar.activation(
                    out=tile[:, t * S : (t + 1) * S], in_=bank[:], func=SIN, bias=bias[:, b, RUN * t : RUN * t + 1]
                )
            sine[b] = tile

        make_sines(0, keep.tile([P, PACK * S], F32, name="sine0", align_bytes=64)[:])

        def quantise(grouped, name):
            width = grouped.shape[1] // PACK
            codes = keep.tile([P, width], U32, name=name + "_codes", align_bytes=64)
            scales = keep.tile([P, width], U8, name=name + "_scales", align_bytes=64)
            nc.vector.quantize_mx(out=codes[:].bitcast(E4M3), scales=scales[:], in_=grouped)
            return codes, scales

        wc_codes = {}
        wo_codes = {}

        def round_wc(copy, a, b, t0, n_slots, grouped):
            copy(
                out=grouped.rearrange("p (t u i j) -> p t u j i", t=n_slots, i=RUN, j=PACK),
                in_=wc_raw[a, b].rearrange("p j (u t i) -> p t u j i", t=PACK, i=RUN)[:, t0 : t0 + n_slots],
            )

        def quantise_tiles(book, key, first_tile, grouped):
            codes, scales = quantise(grouped, "q%s_%d" % ("".join(str(x) for x in key), first_tile))
            for n_tile in range(grouped.shape[1] // KP):
                cols = slice(n_tile * P, (n_tile + 1) * P)
                book[key[1:] + (first_tile + n_tile,)] = (codes[:, cols], scales[:, cols])

        def round_wo(b, pair, grouped):
            n0 = 2 * P * pair
            nc.scalar.copy(
                out=grouped.rearrange("p (c i t) -> p c t i", i=4, t=PACK),
                in_=wo_raw[b][:, :, n0 : n0 + 2 * P].rearrange("p t (c i) -> p c t i", i=4),
            )

        def products(b, js, slots, first):
            width = BANK // len(slots)
            banks = [psum.tile([P, BANK], F32, name=nm) for nm in ("first", "second")]
            for n_list in range(2):
                for n_slot, t in enumerate(slots):
                    for a in range(2):
                        codes, scales = wc_codes[a, b, t]
                        nc.tensor.matmul_mx(
                            out=banks[n_list][:, n_slot * width : (n_slot + 1) * width],
                            lhsT=codes.bitcast(E4M3),
                            lhsT_scale=scales,
                            rhs=picked[n_list, a][:, js].bitcast(E4M3),
                            rhs_scale=picked_planes[n_list][4 * a : P, js],
                            start=(a == 0),
                            stop=(a == 1),
                        )
            nc.scalar.copy(out=first, in_=banks[0][:])
            return banks[1], first

        def take(op, target, n_unit, made):
            mine = slice(n_unit * BANK, (n_unit + 1) * BANK)
            nc.vector.tensor_tensor(out=target[:, mine], in0=made[0][:], in1=made[1], op=op)

        def turn(engine, larger, n_unit, b, js, slots):
            mine = larger[:, n_unit * BANK : (n_unit + 1) * BANK].rearrange("p (t j) -> p t j", t=len(slots))
            factor = sine[b].rearrange("p (t j) -> p t j", t=PACK)[:, slots[0] : slots[-1] + 1, js]
            engine.tensor_tensor(out=mine, in0=mine, in1=factor, op=ALU.mult)

        def join(larger, smaller, width):
            grouped = keep.tile([P, PACK * width], BF16, name="h_grouped", tag="h%d" % smaller.shape[1], bufs=1 if width > P else 2, align_bytes=64)
            nc.vector.tensor_tensor(
                out=grouped[:].rearrange("p (c i t) -> p c t i", i=2, t=PACK),
                in0=larger[:, 0 : PACK * width].rearrange("p (t c i) -> p c t i", t=PACK, i=2),
                in1=smaller[:].rearrange("p (t c i) -> p c t i", t=PACK, i=2),
                op=ALU.add,
            )
            return grouped

        def project(j0, width, h_low, h_high, last):
            per_bank = 2 if width == 256 else 3
            js = slice(j0, j0 + width)
            halves = ((h_low[0][:, js], h_low[1][:, js]), (h_high[0][:], h_high[1][:]))
            for n_bank in range(N // P // per_bank):
                bank = psum.tile([P, per_bank, width], F32, name="result", tag="node" if last else "result")
                for b in range(2):
                    for n_slot in range(per_bank):
                        codes, scales = wo_codes[b, n_bank * per_bank + n_slot]
                        nc.tensor.matmul_mx(
                            out=bank[:, n_slot, :],
                            lhsT=codes.bitcast(E4M3),
                            lhsT_scale=scales,
                            rhs=halves[b][0].bitcast(E4M3),
                            rhs_scale=halves[b][1],
                            start=(b == 0 and n_slot == 0),
                            stop=(b == 1 and n_slot == per_bank - 1),
                        )
                staged = ring.tile([P, per_bank, width], F32, name="staged", bufs=7)
                if last and n_bank == 0:
                    nc.vector.tensor_copy(out=staged[:], in_=bank[:])
                else:
                    nc.scalar.copy(out=staged[:], in_=bank[:])
                rows = slice(n_bank * per_bank * P, (n_bank + 1) * per_bank * P)
                nc.sync.dma_start(out=out[rows, js].rearrange("(s p) j -> p s j", p=P), in_=staged[:])

        all_slots = tuple(range(PACK))
        whole = slice(0, S)

        early = keep.tile([P, 2, PACK * KP], BF16, name="early", tag="table1", align_bytes=64)

        def early_part(a, t0, n_slots):
            return early[:, a, t0 * KP : (t0 + n_slots) * KP]

        round_wc(nc.scalar.copy, 0, 0, 2, 2, early_part(0, 2, 2))
        round_wc(nc.vector.tensor_copy, 0, 0, 0, 2, early_part(0, 0, 2))
        round_wc(nc.vector.tensor_copy, 1, 0, 0, 1, early_part(1, 0, 1))
        quantise_tiles(wc_codes, ("c", 0, 0), 0, early_part(0, 0, 2))
        quantise_tiles(wc_codes, ("c", 1, 0), 0, early_part(1, 0, 1))
        round_wc(nc.vector.tensor_copy, 1, 0, 1, 1, early_part(1, 1, 1))
        round_wc(nc.vector.tensor_copy, 1, 0, 2, 2, early_part(1, 2, 2))
        quantise_tiles(wc_codes, ("c", 1, 0), 1, early_part(1, 1, 1))
        quantise_tiles(wc_codes, ("c", 0, 0), 2, early_part(0, 2, 2))
        quantise_tiles(wc_codes, ("c", 1, 0), 2, early_part(1, 2, 2))

        firsts = [keep.tile([P, 2 * BANK], F32, name="first%d" % n, align_bytes=64) for n in range(4)]

        def first_of(n_unit):
            return firsts[n_unit // 2][:, (n_unit % 2) * BANK : (n_unit % 2 + 1) * BANK]

        larger = keep.tile([P, PACK * S], F32, name="larger")
        smaller = keep.tile([P, PACK * S], F32, name="smaller0")
        for t in range(PACK):
            made = products(0, whole, (t,), first_of(t))
            take(ALU.max, larger, t, made)
            take(ALU.min, smaller, t, made)
            turn(nc.gpsimd if t < 3 else nc.vector, larger, t, 0, whole, (t,))
            copy = nc.scalar.copy if t < 3 else nc.vector.tensor_copy
            round_wc(copy, t // 2, 1, 2 * (t % 2), 2, first_of(t).bitcast(BF16))
        make_sines(1, shared[:, 0 : PACK * S])
        for a in range(2):
            quantise_tiles(wc_codes, ("c", a, 1), 0, firsts[a][:].bitcast(BF16))
        grouped_low = join(larger, smaller, S)

        wide = slice(0, 256)
        mid = slice(256, 384)
        end = slice(384, 512)
        smaller = keep.tile([P, PACK * 256], F32, name="smaller1")
        smaller_mid = keep.tile([P, BANK], F32, name="smaller_mid")
        smaller_end = keep.tile([P, BANK], F32, name="smaller_end")
        larger_end = keep.tile([P, BANK], F32, name="larger_end")
        made = products(1, wide, (0, 1), first_of(4))
        take(ALU.min, smaller, 0, made)
        h_low = quantise(grouped_low[:], "h0")
        take(ALU.max, larger, 0, made)
        turn(nc.gpsimd, larger, 0, 1, wide, (0, 1))
        made = products(1, wide, (2, 3), first_of(5))
        take(ALU.max, larger, 1, made)
        take(ALU.min, smaller, 1, made)
        made_mid = products(1, mid, all_slots, first_of(6))
        made_end = products(1, end, all_slots, first_of(7))
        wo_low = sine[0].bitcast(BF16)
        for pair in range(3):
            round_wo(0, pair, wo_low[:, pair * 2 * KP : (pair + 1) * 2 * KP])
        wo_high = [grouped_low[:, 0 : 2 * KP], grouped_low[:, 2 * KP : 4 * KP], first_of(4).bitcast(BF16)]
        for pair in range(3):
            round_wo(1, pair, wo_high[pair])
        turn(nc.vector, larger, 1, 1, wide, (2, 3))
        take(ALU.min, smaller_mid, 0, made_mid)
        grouped = join(larger, smaller, 256)
        quantise_tiles(wo_codes, ("o", 0), 0, wo_low[:, 0 : 4 * KP])
        quantise_tiles(wo_codes, ("o", 0), 4, wo_low[:, 4 * KP : 6 * KP])
        h_wide = quantise(grouped[:], "h_wide")
        quantise_tiles(wo_codes, ("o", 1), 0, grouped_low[:])
        quantise_tiles(wo_codes, ("o", 1), 4, wo_high[2])
        project(0, 256, h_low, h_wide, False)
        take(ALU.max, larger, 0, made_mid)
        turn(nc.gpsimd, larger, 0, 1, mid, all_slots)
        take(ALU.max, larger_end, 0, made_end)
        take(ALU.min, smaller_end, 0, made_end)
        grouped = join(larger, smaller_mid, P)
        turn(nc.vector, larger_end, 0, 1, end, all_slots)
        h_mid = quantise(grouped[:], "h_mid")
        project(mid.start, P, h_low, h_mid, False)
        grouped_end = join(larger_end, smaller_end, P)
        h_end = quantise(grouped_end[:], "h_end")
        project(end.start, P, h_low, h_end, True)
